import numpy as np
import ml_dtypes


def mxq(x, axis, fmt="e4m3"):
    dtype, down = {"e4m3": (ml_dtypes.float8_e4m3fn, 7), "e5m2": (ml_dtypes.float8_e5m2, 14)}[fmt]
    v = np.moveaxis(np.asarray(x, np.float32).astype(ml_dtypes.bfloat16).astype(np.float64), axis, -1)
    blocks = v.reshape(v.shape[:-1] + (-1, 32))
    amax = np.abs(blocks).max(-1, keepdims=True)
    byte = np.maximum(np.where(amax > 0, np.frexp(amax)[1] - 1 + 127, 0) - down, 1)
    scale = np.exp2(byte - 127.0)
    codes = (blocks / scale).astype(np.float32).astype(dtype).astype(np.float64)
    return np.moveaxis((codes * scale).reshape(v.shape), -1, axis)


WIDE = False


def mx_kscale(k):
    if not WIDE:
        return np.ones(k)
    levels = np.array([10, -10, 5, -5, 0])
    if k % 512:
        return np.exp2(np.random.permutation(np.resize(levels, k // 32))).repeat(32)
    a = np.empty((k // 512, 16))
    for p in range(k // 512):
        a[p, :8] = np.random.permutation(np.resize(levels, 8))
        for g in range(8):
            far = levels[np.abs(levels - a[p, g]) >= 10]
            a[p, g + 8] = far[np.random.randint(len(far))]
    return np.exp2(a.ravel()).repeat(32)


def f64(x):
    return np.asarray(x).astype(np.float64)


def striped8(idx):
    return np.asarray(idx).reshape(8, -1, 16).transpose(0, 2, 1).reshape(128, -1).astype(np.uint16)


def unstriped8(offs):
    return offs.reshape(8, 16, -1).transpose(0, 2, 1).reshape(8, -1).astype(np.int64)


def pick8(x, idx, run):
    r = np.arange(len(x))
    return x[r[:, None], idx[r % (8 * run) // run]]


E2M1 = np.array([0.0, 0.5, 1.0, 1.5, 2.0, 3.0, 4.0, 6.0, -0.0, -0.5, -1.0, -1.5, -2.0, -3.0, -4.0, -6.0])


def pack_weight(w, fmt):
    k, n = w.shape
    w = f64(np.asarray(w, np.float32).astype(ml_dtypes.bfloat16)).reshape(k // 32, 32, n)
    amax = np.abs(w).max(1)
    if fmt == "e4m3":
        byte = np.frexp(amax)[1] - 1 + 127 - 7
    else:
        mant, ex = np.frexp(amax / 6.0)
        byte = np.where(mant > 0.5, ex, ex - 1) + 127
    byte = np.clip(np.where(amax > 0, byte, 1), 1, 254)
    scaled = (w * np.exp2(127.0 - byte)[:, None, :]).reshape(k, n).astype(np.float32)
    by_word = np.ascontiguousarray(scaled.reshape(k // 512, 128, 4, n).transpose(0, 1, 3, 2))
    if fmt == "e4m3":
        words = by_word.astype(ml_dtypes.float8_e4m3fn).view(np.uint8)
    else:
        c = by_word.astype(ml_dtypes.float4_e2m1fn).view(np.uint8) & 0xF
        words = (c[..., 0::2] | (c[..., 1::2] << 4)).reshape(k // 512, 128, 2 * n)
    return np.ascontiguousarray(words), np.ascontiguousarray(byte.astype(np.uint8).reshape(k // 512, 16, n))


def unpack_weight(words, scales, fmt):
    g, _, n = scales.shape
    words = np.ascontiguousarray(words).reshape(g, 128, n, -1)
    if fmt == "e4m3":
        vals = words.view(ml_dtypes.float8_e4m3fn).astype(np.float64)
    else:
        nib = np.empty((g, 128, n, 4), np.uint8)
        nib[..., 0::2] = words & 0xF
        nib[..., 1::2] = words >> 4
        vals = E2M1[nib]
    vals = vals * np.repeat(np.exp2(scales.astype(np.float64) - 127.0), 8, axis=1)[..., None]
    return vals.transpose(0, 1, 3, 2).reshape(g * 512, n)


D, E, T, Q, I = 512, 512, 1024, 128, 512


def setup_inputs():
    n = np.random.standard_normal
    idx = np.stack([np.random.permutation(T)[:I] for _ in range(8)])
    fd = mx_kscale(D)
    ft = mx_kscale(T)
    keysp = pack_weight(n((D, T)) / fd[:, None], "e2m1")
    return {
        "query": (n((D, Q)) * 1.0 / np.sqrt(D) * fd[:, None]).astype(np.float32),
        "keys_words": keysp[0],
        "keys_scales": keysp[1],
        "th": (np.random.uniform(-0.5, 0.5, (Q, 1))).astype(np.float32),
        "reserve": (np.random.uniform(20.0, 60.0, (Q, 1))).astype(np.float32),
        "ground": (np.random.uniform(0.0, 0.004, (Q, T))).astype(np.float32),
        "fac": (np.random.uniform(8.0, 32.0, (1, T)) * ft).astype(np.float32),
        "vals": (n((T, E)) / ft[:, None]).astype(np.float32),
        "offs": striped8(idx),
    }


def reference(query, keys_words, keys_scales, th, reserve, ground, fac, vals, offs):
    idx = unstriped8(offs)
    keysu = unpack_weight(keys_words, keys_scales, "e2m1")
    queryq = mxq(f64(query), 0, "e4m3")
    a = queryq.T @ keysu
    b = np.maximum(pick8(a, idx, 16) - f64(th), 0.0)
    u = b / (np.sum(b, axis=1, keepdims=True) + f64(reserve))
    uf = np.zeros((Q, T))
    uf[np.arange(Q)[:, None], idx[np.arange(Q) % 128 // 16]] = u
    wg = (uf + f64(ground)) * f64(fac)
    wt = wg.T
    wtq = mxq(wt, 0, "e4m3")
    valsq = mxq(f64(vals), 0, "e4m3")
    o = wtq.T @ valsq
    return o

@@ -1,0 +1,165 @@
+from contextlib import ExitStack
+
+import concourse.mybir as mybir
+from concourse.masks import make_identity
+
+D, E, T, Q, SLOTS = 512, 512, 1024, 128, 512
+FLOPS = 2 * Q * D * T + 2 * Q * T * E
+
+F32 = mybir.dt.float32
+BF16 = mybir.dt.bfloat16
+I32 = mybir.dt.int32
+U32 = mybir.dt.uint32
+U16 = mybir.dt.uint16
+U8 = mybir.dt.uint8
+FP8X4 = mybir.dt.float8_e4m3fn_x4
+FP4X4 = mybir.dt.float4_e2m1fn_x4
+ALU = mybir.AluOpType
+ACT = mybir.ActivationFunctionType
+
+P = 128
+PACK = 4
+K_PASS = P * PACK
+PASSES = T // K_PASS
+SCORE_N = 256
+E_HALF = E // 2
+HALF = SLOTS // 2
+
+
+def interleave_views(grouped, raw):
+    return (grouped[:].rearrange("p (c i) t -> p c t i", i=4), raw[:].rearrange("p t (c i) -> p c t i", i=4))
+
+
+def tile_attend_spotlight_heads_kernel(tc, query, keys_words, keys_scales, th, reserve, ground, fac, vals, offs, out):
+    nc = tc.nc
+    with ExitStack() as ctx:
+        sb = ctx.enter_context(tc.tile_pool(name="sb", bufs=1))
+        ps = ctx.enter_context(tc.psum_pool(name="ps", bufs=1))
+
+        offsets = sb.tile([P, SLOTS // 16], U16, name="offsets")
+        q_raw = sb.tile([P, PACK, Q], F32, name="q_raw")
+        k_words = sb.tile([P, 2 * T], U8, name="k_words", align_bytes=64)
+        k_scales = sb.tile([P, T], U8, name="k_scales", align_bytes=64)
+        th_sb = sb.tile([P, 1], F32, name="th_sb")
+        res_sb = sb.tile([P, 1], F32, name="res_sb")
+        fac_sb = sb.tile([P, PASSES, PACK], F32, name="fac_sb")
+        ground_sb = sb.tile([P, T], F32, name="ground_sb")
+        v_raw = {(g, h): sb.tile([P, PACK, E_HALF], F32, name="v_raw_%d_%d" % (g, h)) for g in range(PASSES) for h in range(2)}
+        placed = sb.tile([P, T], F32, name="placed")
+        ident = sb.tile([P, P], F32, name="ident")
+
+        nc.vector.memset(k_scales[:].bitcast(I32), 0)
+        nc.vector.memset(placed[:], 0.0)
+
+        def load_vals(g, h):
+            rows = vals[g * K_PASS:(g + 1) * K_PASS, h * E_HALF:(h + 1) * E_HALF]
+            nc.sync.dma_start(out=v_raw[g, h][:], in_=rows.rearrange("(p j) e -> p j e", j=PACK))
+
+        nc.sync.dma_start(out=q_raw[:], in_=query.rearrange("(p j) q -> p j q", j=PACK))
+        for quad in range(4):
+            nc.scalar.dma_start(out=k_scales[32 * quad:32 * quad + 4, :].bitcast(I32), in_=keys_scales[0, 4 * quad:4 * quad + 4, :].bitcast(I32))
+        nc.sync.dma_start(out=k_words[:].bitcast(I32), in_=keys_words[0].bitcast(I32))
+        nc.sync.dma_start(offsets[:], offs)
+        load_vals(0, 0)
+        nc.sync.dma_start(out=th_sb[:], in_=th)
+        load_vals(0, 1)
+        nc.sync.dma_start(out=res_sb[:], in_=reserve)
+        nc.sync.dma_start(out=ground_sb[:], in_=ground)
+        nc.sync.dma_start(out=fac_sb[:], in_=fac.rearrange("o (g p r) -> p (o g) r", p=P, r=PACK))
+        load_vals(1, 0)
+        load_vals(1, 1)
+        make_identity(nc, ident[:])
+
+        neg_th = sb.tile([P, 1], F32, name="neg_th")
+        warm = sb.tile([P, 1], F32, name="warm")
+        nc.scalar.activation(out=warm[:], in_=ident[:, 0:1], func=ACT.Relu)
+        nc.gpsimd.tensor_scalar(out=neg_th[:], in0=th_sb[:], scalar1=-1.0, scalar2=0.0, op0=ALU.mult, op1=ALU.add)
+
+        q_bf = sb.tile([P, Q, PACK], BF16, name="q_bf", align_bytes=64)
+        q_codes = sb.tile([P, Q], U32, name="q_codes", align_bytes=64)
+        q_scales = sb.tile([P, Q], U8, name="q_scales", align_bytes=64)
+        dst, src = interleave_views(q_bf, q_raw)
+        nc.vector.tensor_copy(out=dst, in_=src)
+        nc.vector.quantize_mx(out=q_codes[:].bitcast(FP8X4), scales=q_scales[:], in_=q_bf[:].rearrange("p q j -> p (q j)"))
+
+        a = sb.tile([P, T], F32, name="a")
+        for n in range(T // SCORE_N):
+            bank = ps.tile([P, SCORE_N], F32, name="score_%d" % n)
+            nc.tensor.matmul_mx(
+                out=bank[:], lhsT=q_codes[:].bitcast(FP8X4), lhsT_scale=q_scales[:],
+                rhs=k_words[:, 2 * n * SCORE_N:2 * (n + 1) * SCORE_N].bitcast(FP4X4),
+                rhs_scale=k_scales[:, n * SCORE_N:(n + 1) * SCORE_N], start=True, stop=True)
+            if n % 2 == 0:
+                nc.scalar.copy(out=a[:, n * SCORE_N:(n + 1) * SCORE_N], in_=bank[:])
+            else:
+                nc.vector.tensor_copy(out=a[:, n * SCORE_N:(n + 1) * SCORE_N], in_=bank[:])
+
+        lists = [offsets[:, s * (HALF // 16):(s + 1) * (HALF // 16)] for s in range(2)]
+        picked = [sb.tile([P, HALF], F32, name="picked_%d" % s) for s in range(2)]
+        b = [sb.tile([P, HALF], F32, name="b_%d" % s) for s in range(2)]
+        sums = [sb.tile([P, 1], F32, name="sum_%d" % s) for s in range(2)]
+        for s in range(2):
+            nc.vector.tensor_copy(out=picked[s][:], in_=a[:].indirect(lists[s]))
+        for s in range(2):
+            nc.scalar.activation(out=b[s][:], in_=picked[s][:], func=ACT.Relu, bias=neg_th[:], accum_out=sums[s][:])
+        den = sb.tile([P, 1], F32, name="den")
+        inv = sb.tile([P, 1], F32, name="inv")
+        nc.vector.tensor_copy(out=placed[:].indirect(lists[0]), in_=b[0][:])
+        nc.vector.tensor_scalar(out=den[:], in0=sums[0][:], scalar1=sums[1][:], scalar2=res_sb[:], op0=ALU.add, op1=ALU.add)
+        nc.vector.tensor_copy(out=placed[:].indirect(lists[1]), in_=b[1][:])
+        nc.vector.reciprocal(out=inv[:], in_=den[:])
+
+        wt_bank = [ps.tile([P, PACK, Q], F32, name="wt_bank_%d" % g) for g in range(PASSES)]
+        for g in range(PASSES):
+            for r in range(PACK):
+                nc.tensor.matmul(wt_bank[g][:, r, :], ground_sb[:, g * K_PASS + r:(g + 1) * K_PASS:PACK], ident[:],
+                                 start=(r == 0), stop=False, is_transpose=True)
+
+        v_bf, v_codes, v_scales = {}, {}, {}
+        for g in range(PASSES):
+            for h in range(2):
+                v_bf[g, h] = sb.tile([P, E_HALF, PACK], BF16, name="v_bf_%d_%d" % (g, h), align_bytes=64)
+                v_codes[g, h] = sb.tile([P, E_HALF], U32, name="v_codes_%d_%d" % (g, h), align_bytes=64)
+                v_scales[g, h] = sb.tile([P, E_HALF], U8, name="v_scales_%d_%d" % (g, h), align_bytes=64)
+                dst, src = interleave_views(v_bf[g, h], v_raw[g, h])
+                nc.scalar.copy(out=dst, in_=src)
+
+        def quantize_vals(g, h):
+            nc.vector.quantize_mx(out=v_codes[g, h][:].bitcast(FP8X4), scales=v_scales[g, h][:], in_=v_bf[g, h][:].rearrange("p e j -> p (e j)"))
+
+        dealt = [sb.tile([P, PACK, P], F32, name="dealt_%d" % g) for g in range(PASSES)]
+        for g in range(PASSES):
+            dst = dealt[g][:].rearrange("q r (c i) -> q c r i", i=4)
+            src = placed[:, g * K_PASS:(g + 1) * K_PASS].rearrange("q (c i r) -> q c r i", i=4, r=PACK)
+            if g == 0:
+                nc.vector.tensor_scalar(out=dst, in0=src, scalar1=inv[:], scalar2=None, op0=ALU.mult)
+            else:
+                nc.scalar.activation(out=dst, in_=src, func=ACT.Copy, scale=inv[:])
+            for r in range(PACK):
+                nc.tensor.matmul(wt_bank[g][:, r, :], dealt[g][:, r, :], ident[:],
+                                 start=False, stop=(r == PACK - 1), is_transpose=True)
+        for h in range(2):
+            quantize_vals(0, h)
+
+        w_bf = [sb.tile([P, Q, PACK], BF16, name="w_bf_%d" % g, align_bytes=64) for g in range(PASSES)]
+        w_codes = [sb.tile([P, Q], U32, name="w_codes_%d" % g, align_bytes=64) for g in range(PASSES)]
+        w_scales = [sb.tile([P, Q], U8, name="w_scales_%d" % g, align_bytes=64) for g in range(PASSES)]
+        for g in range(PASSES):
+            nc.vector.tensor_tensor(out=w_bf[g][:], in0=wt_bank[g][:].rearrange("p r q -> p q r"),
+                                    in1=fac_sb[:, g, :].unsqueeze(1).to_broadcast([P, Q, PACK]), op=ALU.mult)
+        out_bank = [ps.tile([P, E_HALF], F32, name="out_bank_%d" % h) for h in range(2)]
+        for g in range(PASSES):
+            nc.vector.quantize_mx(out=w_codes[g][:].bitcast(FP8X4), scales=w_scales[g][:], in_=w_bf[g][:].rearrange("p q j -> p (q j)"))
+            if g == 0:
+                for h in range(2):
+                    quantize_vals(1, h)
+            for h in range(2):
+                nc.tensor.matmul_mx(
+                    out=out_bank[h][:], lhsT=w_codes[g][:].bitcast(FP8X4), lhsT_scale=w_scales[g][:],
+                    rhs=v_codes[g, h][:].bitcast(FP8X4), rhs_scale=v_scales[g, h][:],
+                    start=(g == 0), stop=(g == PASSES - 1))
+        result = [sb.tile([P, E_HALF], F32, name="result_%d" % h) for h in range(2)]
+        nc.scalar.copy(out=result[0][:], in_=out_bank[0][:])
+        nc.vector.tensor_copy(out=result[1][:], in_=out_bank[1][:])
+        nc.scalar.dma_start(out=out[:, 0:E_HALF], in_=result[0][:])
+        nc.sync.dma_start(out=out[:, E_HALF:E], in_=result[1][:])

@@ -21,7 +21,7 @@ P = 128
 PACK = 4
 K_PASS = P * PACK
 PASSES = T // K_PASS
-SCORE_N = 256
+SCORE_WIDTHS = (256, 256, 256, 128, 128)
 E_HALF = E // 2
 HALF = SLOTS // 2
 
@@ -38,17 +38,17 @@ def tile_attend_spotlight_heads_kernel(tc, query, keys_words, keys_scales, th, r
 
         offsets = sb.tile([P, SLOTS // 16], U16, name="offsets")
         q_raw = sb.tile([P, PACK, Q], F32, name="q_raw")
-        k_words = sb.tile([P, 2 * T], U8, name="k_words", align_bytes=64)
+        k_words = sb.tile([P, 2 * T], U8, name="k_words", tag="k_words", align_bytes=64)
         k_scales = sb.tile([P, T], U8, name="k_scales", align_bytes=64)
         th_sb = sb.tile([P, 1], F32, name="th_sb")
         res_sb = sb.tile([P, 1], F32, name="res_sb")
         fac_sb = sb.tile([P, PASSES, PACK], F32, name="fac_sb")
-        ground_sb = sb.tile([P, T], F32, name="ground_sb")
-        v_raw = {(g, h): sb.tile([P, PACK, E_HALF], F32, name="v_raw_%d_%d" % (g, h)) for g in range(PASSES) for h in range(2)}
+        ground_sb = [sb.tile([P, K_PASS], F32, name="ground_%d" % g) for g in range(PASSES)]
+        v_raw = {(g, h): sb.tile([P, PACK, E_HALF], F32, name="v_raw_%d_%d" % (g, h), tag="v_raw_%d_%d" % (g, h), align_bytes=64) for g in range(PASSES) for h in range(2)}
         placed = sb.tile([P, T], F32, name="placed")
         ident = sb.tile([P, P], F32, name="ident")
 
-        nc.vector.memset(k_scales[:].bitcast(I32), 0)
+        nc.gpsimd.memset(k_scales[:].bitcast(I32), 0)
         nc.vector.memset(placed[:], 0.0)
 
         def load_vals(g, h):
@@ -57,14 +57,15 @@ def tile_attend_spotlight_heads_kernel(tc, query, keys_words, keys_scales, th, r
 
         nc.sync.dma_start(out=q_raw[:], in_=query.rearrange("(p j) q -> p j q", j=PACK))
         for quad in range(4):
-            nc.scalar.dma_start(out=k_scales[32 * quad:32 * quad + 4, :].bitcast(I32), in_=keys_scales[0, 4 * quad:4 * quad + 4, :].bitcast(I32))
-        nc.sync.dma_start(out=k_words[:].bitcast(I32), in_=keys_words[0].bitcast(I32))
+            nc.sync.dma_start(out=k_scales[32 * quad:32 * quad + 4, :].bitcast(I32), in_=keys_scales[0, 4 * quad:4 * quad + 4, :].bitcast(I32))
+        nc.scalar.dma_start(out=k_words[:].bitcast(I32), in_=keys_words[0].bitcast(I32))
         nc.sync.dma_start(offsets[:], offs)
         load_vals(0, 0)
         nc.sync.dma_start(out=th_sb[:], in_=th)
+        nc.sync.dma_start(out=ground_sb[0][:], in_=ground[:, 0:K_PASS])
         load_vals(0, 1)
         nc.sync.dma_start(out=res_sb[:], in_=reserve)
-        nc.sync.dma_start(out=ground_sb[:], in_=ground)
+        nc.sync.dma_start(out=ground_sb[1][:], in_=ground[:, K_PASS:T])
         nc.sync.dma_start(out=fac_sb[:], in_=fac.rearrange("o (g p r) -> p (o g) r", p=P, r=PACK))
         load_vals(1, 0)
         load_vals(1, 1)
@@ -72,7 +73,7 @@ def tile_attend_spotlight_heads_kernel(tc, query, keys_words, keys_scales, th, r
 
         neg_th = sb.tile([P, 1], F32, name="neg_th")
         warm = sb.tile([P, 1], F32, name="warm")
-        nc.scalar.activation(out=warm[:], in_=ident[:, 0:1], func=ACT.Relu)
+        nc.scalar.activation(out=warm[:], in_=placed[:, 0:1], func=ACT.Relu)
         nc.gpsimd.tensor_scalar(out=neg_th[:], in0=th_sb[:], scalar1=-1.0, scalar2=0.0, op0=ALU.mult, op1=ALU.add)
 
         q_bf = sb.tile([P, Q, PACK], BF16, name="q_bf", align_bytes=64)
@@ -83,19 +84,22 @@ def tile_attend_spotlight_heads_kernel(tc, query, keys_words, keys_scales, th, r
         nc.vector.quantize_mx(out=q_codes[:].bitcast(FP8X4), scales=q_scales[:], in_=q_bf[:].rearrange("p q j -> p (q j)"))
 
         a = sb.tile([P, T], F32, name="a")
-        for n in range(T // SCORE_N):
-            bank = ps.tile([P, SCORE_N], F32, name="score_%d" % n)
+        lo = 0
+        for n, width in enumerate(SCORE_WIDTHS):
+            hi = lo + width
+            bank = ps.tile([P, width], F32, name="score_%d" % n, tag="score_%d" % n)
             nc.tensor.matmul_mx(
                 out=bank[:], lhsT=q_codes[:].bitcast(FP8X4), lhsT_scale=q_scales[:],
-                rhs=k_words[:, 2 * n * SCORE_N:2 * (n + 1) * SCORE_N].bitcast(FP4X4),
-                rhs_scale=k_scales[:, n * SCORE_N:(n + 1) * SCORE_N], start=True, stop=True)
-            if n % 2 == 0:
-                nc.scalar.copy(out=a[:, n * SCORE_N:(n + 1) * SCORE_N], in_=bank[:])
+                rhs=k_words[:, 2 * lo:2 * hi].bitcast(FP4X4),
+                rhs_scale=k_scales[:, lo:hi], start=True, stop=True)
+            if n % 2 == 1:
+                nc.scalar.copy(out=a[:, lo:hi], in_=bank[:])
             else:
-                nc.vector.tensor_copy(out=a[:, n * SCORE_N:(n + 1) * SCORE_N], in_=bank[:])
+                nc.vector.tensor_copy(out=a[:, lo:hi], in_=bank[:])
+            lo = hi
 
         lists = [offsets[:, s * (HALF // 16):(s + 1) * (HALF // 16)] for s in range(2)]
-        picked = [sb.tile([P, HALF], F32, name="picked_%d" % s) for s in range(2)]
+        picked = [sb.tile([P, HALF], F32, name="picked_%d" % s, tag="picked_%d" % s, align_bytes=64) for s in range(2)]
         b = [sb.tile([P, HALF], F32, name="b_%d" % s) for s in range(2)]
         sums = [sb.tile([P, 1], F32, name="sum_%d" % s) for s in range(2)]
         for s in range(2):
@@ -103,31 +107,43 @@ def tile_attend_spotlight_heads_kernel(tc, query, keys_words, keys_scales, th, r
         for s in range(2):
             nc.scalar.activation(out=b[s][:], in_=picked[s][:], func=ACT.Relu, bias=neg_th[:], accum_out=sums[s][:])
         den = sb.tile([P, 1], F32, name="den")
-        inv = sb.tile([P, 1], F32, name="inv")
+        inv = sb.tile([P, 1], F32, name="inv", tag="inv", align_bytes=64)
         nc.vector.tensor_copy(out=placed[:].indirect(lists[0]), in_=b[0][:])
-        nc.vector.tensor_scalar(out=den[:], in0=sums[0][:], scalar1=sums[1][:], scalar2=res_sb[:], op0=ALU.add, op1=ALU.add)
         nc.vector.tensor_copy(out=placed[:].indirect(lists[1]), in_=b[1][:])
-        nc.vector.reciprocal(out=inv[:], in_=den[:])
 
         wt_bank = [ps.tile([P, PACK, Q], F32, name="wt_bank_%d" % g) for g in range(PASSES)]
         for g in range(PASSES):
             for r in range(PACK):
-                nc.tensor.matmul(wt_bank[g][:, r, :], ground_sb[:, g * K_PASS + r:(g + 1) * K_PASS:PACK], ident[:],
+                nc.tensor.matmul(wt_bank[g][:, r, :], ground_sb[g][:, r:K_PASS:PACK], ident[:],
                                  start=(r == 0), stop=False, is_transpose=True)
 
-        v_bf, v_codes, v_scales = {}, {}, {}
+        v_codes, v_scales, v_bf = {}, {}, {}
         for g in range(PASSES):
             for h in range(2):
-                v_bf[g, h] = sb.tile([P, E_HALF, PACK], BF16, name="v_bf_%d_%d" % (g, h), align_bytes=64)
                 v_codes[g, h] = sb.tile([P, E_HALF], U32, name="v_codes_%d_%d" % (g, h), align_bytes=64)
                 v_scales[g, h] = sb.tile([P, E_HALF], U8, name="v_scales_%d_%d" % (g, h), align_bytes=64)
-                dst, src = interleave_views(v_bf[g, h], v_raw[g, h])
-                nc.scalar.copy(out=dst, in_=src)
 
-        def quantize_vals(g, h):
-            nc.vector.quantize_mx(out=v_codes[g, h][:].bitcast(FP8X4), scales=v_scales[g, h][:], in_=v_bf[g, h][:].rearrange("p e j -> p (e j)"))
+        def cast_vals(g, h, lo, hi, tag):
+            v_bf[g, h, lo] = sb.tile([P, hi - lo, PACK], BF16, name="v_bf_%d_%d_%d" % (g, h, lo), tag=tag, align_bytes=64)
+            nc.scalar.copy(out=v_bf[g, h, lo][:].rearrange("p (c i) t -> p c t i", i=4),
+                           in_=v_raw[g, h][:, :, lo:hi].rearrange("p t (c i) -> p c t i", i=4))
 
-        dealt = [sb.tile([P, PACK, P], F32, name="dealt_%d" % g) for g in range(PASSES)]
+        def quantize_vals(g, h, lo, hi):
+            nc.vector.quantize_mx(out=v_codes[g, h][:, lo:hi].bitcast(FP8X4), scales=v_scales[g, h][:, lo:hi],
+                                  in_=v_bf[g, h, lo][:].rearrange("p e j -> p (e j)"))
+
+        cast_vals(0, 0, 0, 128, "k_words")
+        cast_vals(0, 0, 128, 256, "picked_1")
+        part = sb.tile([P, 1], F32, name="part")
+        minus_one = sb.tile([P, 1], F32, name="minus_one")
+        nc.gpsimd.memset(minus_one[:], -1.0)
+        nc.gpsimd.tensor_tensor(out=part[:], in0=sums[0][:], in1=res_sb[:], op=ALU.add)
+        nc.scalar.activation(out=den[:], in_=sums[1][:], func=ACT.Identity, bias=part[:])
+        nc.gpsimd.tensor_tensor(out=inv[:], in0=den[:], in1=minus_one[:], op=ALU.pow)
+        cast_vals(0, 1, 0, 256, "picked_0")
+        cast_vals(1, 0, 0, 256, "v_raw_0_0")
+
+        dealt = [sb.tile([P, PACK, P], F32, name="dealt_0"), sb.tile([P, PACK, P], F32, name="dealt_1", tag="v_raw_1_0", align_bytes=64)]
         for g in range(PASSES):
             dst = dealt[g][:].rearrange("q r (c i) -> q c r i", i=4)
             src = placed[:, g * K_PASS:(g + 1) * K_PASS].rearrange("q (c i r) -> q c r i", i=4, r=PACK)
@@ -138,21 +154,23 @@ def tile_attend_spotlight_heads_kernel(tc, query, keys_words, keys_scales, th, r
             for r in range(PACK):
                 nc.tensor.matmul(wt_bank[g][:, r, :], dealt[g][:, r, :], ident[:],
                                  start=False, stop=(r == PACK - 1), is_transpose=True)
-        for h in range(2):
-            quantize_vals(0, h)
+        cast_vals(1, 1, 0, 256, "inv")
+        quantize_vals(0, 0, 0, 128)
+        quantize_vals(0, 0, 128, 256)
+        quantize_vals(0, 1, 0, 256)
+        quantize_vals(1, 0, 0, 256)
 
-        w_bf = [sb.tile([P, Q, PACK], BF16, name="w_bf_%d" % g, align_bytes=64) for g in range(PASSES)]
-        w_codes = [sb.tile([P, Q], U32, name="w_codes_%d" % g, align_bytes=64) for g in range(PASSES)]
+        w_bf = [sb.tile([P, Q, PACK], BF16, name="w_bf_0", tag="picked_0", align_bytes=64), sb.tile([P, Q, PACK], BF16, name="w_bf_1", align_bytes=64)]
+        w_codes = [sb.tile([P, Q], U32, name="w_codes_0", tag="v_raw_1_0", align_bytes=64), sb.tile([P, Q], U32, name="w_codes_1", align_bytes=64)]
         w_scales = [sb.tile([P, Q], U8, name="w_scales_%d" % g, align_bytes=64) for g in range(PASSES)]
         for g in range(PASSES):
             nc.vector.tensor_tensor(out=w_bf[g][:], in0=wt_bank[g][:].rearrange("p r q -> p q r"),
                                     in1=fac_sb[:, g, :].unsqueeze(1).to_broadcast([P, Q, PACK]), op=ALU.mult)
-        out_bank = [ps.tile([P, E_HALF], F32, name="out_bank_%d" % h) for h in range(2)]
+        out_bank = [ps.tile([P, E_HALF], F32, name="out_bank_%d" % h, tag="score_%d" % h) for h in range(2)]
         for g in range(PASSES):
             nc.vector.quantize_mx(out=w_codes[g][:].bitcast(FP8X4), scales=w_scales[g][:], in_=w_bf[g][:].rearrange("p q j -> p (q j)"))
             if g == 0:
-                for h in range(2):
-                    quantize_vals(1, h)
+                quantize_vals(1, 1, 0, 256)
             for h in range(2):
                 nc.tensor.matmul_mx(
                     out=out_bank[h][:], lhsT=w_codes[g][:].bitcast(FP8X4), lhsT_scale=w_scales[g][:],

@@ -34,6 +34,7 @@ def tile_attend_spotlight_heads_kernel(tc, query, keys_words, keys_scales, th, r
     nc = tc.nc
     with ExitStack() as ctx:
         sb = ctx.enter_context(tc.tile_pool(name="sb", bufs=1))
+        reuse = ctx.enter_context(tc.tile_pool(name="reuse", bufs=1))
         ps = ctx.enter_context(tc.psum_pool(name="ps", bufs=1))
 
         offsets = sb.tile([P, SLOTS // 16], U16, name="offsets")
@@ -43,44 +44,44 @@ def tile_attend_spotlight_heads_kernel(tc, query, keys_words, keys_scales, th, r
         th_sb = sb.tile([P, 1], F32, name="th_sb")
         res_sb = sb.tile([P, 1], F32, name="res_sb")
         fac_sb = sb.tile([P, PASSES, PACK], F32, name="fac_sb")
-        ground_sb = [sb.tile([P, K_PASS], F32, name="ground_%d" % g) for g in range(PASSES)]
-        v_raw = {(g, h): sb.tile([P, PACK, E_HALF], F32, name="v_raw_%d_%d" % (g, h), tag="v_raw_%d_%d" % (g, h), align_bytes=64) for g in range(PASSES) for h in range(2)}
+        ground_sb = sb.tile([P, T], F32, name="ground_sb")
+        v_parts = ((0, 0, E), (1, 0, E_HALF), (1, E_HALF, E))
+        v_raw = [sb.tile([P, PACK, E], F32, name="v_raw_0"),
+                 reuse.tile([P, PACK, E_HALF], F32, name="v_raw_1", offset=0, align_bytes=64),
+                 sb.tile([P, PACK, E_HALF], F32, name="v_raw_2")]
         placed = sb.tile([P, T], F32, name="placed")
         ident = sb.tile([P, P], F32, name="ident")
 
         nc.gpsimd.memset(k_scales[:].bitcast(I32), 0)
         nc.vector.memset(placed[:], 0.0)
 
-        def load_vals(g, h):
-            rows = vals[g * K_PASS:(g + 1) * K_PASS, h * E_HALF:(h + 1) * E_HALF]
-            nc.sync.dma_start(out=v_raw[g, h][:], in_=rows.rearrange("(p j) e -> p j e", j=PACK))
+        def load_vals(n):
+            g, lo, hi = v_parts[n]
+            nc.sync.dma_start(out=v_raw[n][:], in_=vals[g * K_PASS:(g + 1) * K_PASS, lo:hi].rearrange("(p j) e -> p j e", j=PACK))
 
         nc.sync.dma_start(out=q_raw[:], in_=query.rearrange("(p j) q -> p j q", j=PACK))
+        nc.sync.dma_start(out=k_words[:].bitcast(I32), in_=keys_words[0].bitcast(I32))
         for quad in range(4):
             nc.sync.dma_start(out=k_scales[32 * quad:32 * quad + 4, :].bitcast(I32), in_=keys_scales[0, 4 * quad:4 * quad + 4, :].bitcast(I32))
-        nc.scalar.dma_start(out=k_words[:].bitcast(I32), in_=keys_words[0].bitcast(I32))
         nc.sync.dma_start(offsets[:], offs)
-        load_vals(0, 0)
+        load_vals(0)
         nc.sync.dma_start(out=th_sb[:], in_=th)
-        nc.sync.dma_start(out=ground_sb[0][:], in_=ground[:, 0:K_PASS])
-        load_vals(0, 1)
         nc.sync.dma_start(out=res_sb[:], in_=reserve)
-        nc.sync.dma_start(out=ground_sb[1][:], in_=ground[:, K_PASS:T])
+        nc.sync.dma_start(out=ground_sb[:], in_=ground)
+        load_vals(1)
+        load_vals(2)
         nc.sync.dma_start(out=fac_sb[:], in_=fac.rearrange("o (g p r) -> p (o g) r", p=P, r=PACK))
-        load_vals(1, 0)
-        load_vals(1, 1)
         make_identity(nc, ident[:])
 
         neg_th = sb.tile([P, 1], F32, name="neg_th")
-        warm = sb.tile([P, 1], F32, name="warm")
-        nc.scalar.activation(out=warm[:], in_=placed[:, 0:1], func=ACT.Relu)
         nc.gpsimd.tensor_scalar(out=neg_th[:], in0=th_sb[:], scalar1=-1.0, scalar2=0.0, op0=ALU.mult, op1=ALU.add)
 
         q_bf = sb.tile([P, Q, PACK], BF16, name="q_bf", align_bytes=64)
         q_codes = sb.tile([P, Q], U32, name="q_codes", align_bytes=64)
         q_scales = sb.tile([P, Q], U8, name="q_scales", align_bytes=64)
         dst, src = interleave_views(q_bf, q_raw)
-        nc.vector.tensor_copy(out=dst, in_=src)
+        nc.vector.tensor_copy(out=dst[:, 0:14], in_=src[:, 0:14])
+        nc.scalar.activation(out=dst[:, 14:32], in_=src[:, 14:32], func=ACT.Copy)
         nc.vector.quantize_mx(out=q_codes[:].bitcast(FP8X4), scales=q_scales[:], in_=q_bf[:].rearrange("p q j -> p (q j)"))
 
         a = sb.tile([P, T], F32, name="a")
@@ -92,7 +93,7 @@ def tile_attend_spotlight_heads_kernel(tc, query, keys_words, keys_scales, th, r
                 out=bank[:], lhsT=q_codes[:].bitcast(FP8X4), lhsT_scale=q_scales[:],
                 rhs=k_words[:, 2 * lo:2 * hi].bitcast(FP4X4),
                 rhs_scale=k_scales[:, lo:hi], start=True, stop=True)
-            if n % 2 == 1:
+            if n not in (0, 2):
                 nc.scalar.copy(out=a[:, lo:hi], in_=bank[:])
             else:
                 nc.vector.tensor_copy(out=a[:, lo:hi], in_=bank[:])
@@ -100,33 +101,41 @@ def tile_attend_spotlight_heads_kernel(tc, query, keys_words, keys_scales, th, r
 
         lists = [offsets[:, s * (HALF // 16):(s + 1) * (HALF // 16)] for s in range(2)]
         picked = [sb.tile([P, HALF], F32, name="picked_%d" % s, tag="picked_%d" % s, align_bytes=64) for s in range(2)]
-        b = [sb.tile([P, HALF], F32, name="b_%d" % s) for s in range(2)]
-        sums = [sb.tile([P, 1], F32, name="sum_%d" % s) for s in range(2)]
+        b = [sb.tile([P, HALF], F32, name="b_%d" % s, tag="b_%d" % s, align_bytes=64) for s in range(2)]
+        sums = [sb.tile([P, 1], F32, name="sum_%d" % s, tag="sum_%d" % s, align_bytes=64) for s in range(2)]
         for s in range(2):
             nc.vector.tensor_copy(out=picked[s][:], in_=a[:].indirect(lists[s]))
+        den = res_sb
         for s in range(2):
             nc.scalar.activation(out=b[s][:], in_=picked[s][:], func=ACT.Relu, bias=neg_th[:], accum_out=sums[s][:])
-        den = sb.tile([P, 1], F32, name="den")
+            so_far, den = den, sb.tile([P, 1], F32, name="den_%d" % s, tag="den_%d" % s, align_bytes=64)
+            nc.scalar.activation(out=den[:], in_=sums[s][:], func=ACT.Identity, bias=so_far[:])
+        minus_one = sb.tile([P, 1], F32, name="minus_one")
+        nc.gpsimd.memset(minus_one[:], -1.0)
         inv = sb.tile([P, 1], F32, name="inv", tag="inv", align_bytes=64)
+        nc.gpsimd.tensor_tensor(out=inv[:], in0=den[:], in1=minus_one[:], op=ALU.pow)
         nc.vector.tensor_copy(out=placed[:].indirect(lists[0]), in_=b[0][:])
         nc.vector.tensor_copy(out=placed[:].indirect(lists[1]), in_=b[1][:])
 
         wt_bank = [ps.tile([P, PACK, Q], F32, name="wt_bank_%d" % g) for g in range(PASSES)]
         for g in range(PASSES):
             for r in range(PACK):
-                nc.tensor.matmul(wt_bank[g][:, r, :], ground_sb[g][:, r:K_PASS:PACK], ident[:],
+                nc.tensor.matmul(wt_bank[g][:, r, :], ground_sb[:, g * K_PASS + r:(g + 1) * K_PASS:PACK], ident[:],
                                  start=(r == 0), stop=False, is_transpose=True)
 
         v_codes, v_scales, v_bf = {}, {}, {}
         for g in range(PASSES):
             for h in range(2):
-                v_codes[g, h] = sb.tile([P, E_HALF], U32, name="v_codes_%d_%d" % (g, h), align_bytes=64)
                 v_scales[g, h] = sb.tile([P, E_HALF], U8, name="v_scales_%d_%d" % (g, h), align_bytes=64)
+
+        v_codes[0, 0] = sb.tile([P, E_HALF], U32, name="v_codes_0_0", tag="den_1", align_bytes=64)
+        v_codes[0, 1] = sb.tile([P, E_HALF], U32, name="v_codes_0_1", align_bytes=64)
+        v_codes[1, 0] = sb.tile([P, E_HALF], U32, name="v_codes_1_0", align_bytes=64)
 
         def cast_vals(g, h, lo, hi, tag):
             v_bf[g, h, lo] = sb.tile([P, hi - lo, PACK], BF16, name="v_bf_%d_%d_%d" % (g, h, lo), tag=tag, align_bytes=64)
             nc.scalar.copy(out=v_bf[g, h, lo][:].rearrange("p (c i) t -> p c t i", i=4),
-                           in_=v_raw[g, h][:, :, lo:hi].rearrange("p t (c i) -> p c t i", i=4))
+                           in_=(v_raw[0][:, :, h * E_HALF + lo:h * E_HALF + hi] if g == 0 else v_raw[1 + h][:]).rearrange("p t (c i) -> p c t i", i=4))
 
         def quantize_vals(g, h, lo, hi):
             nc.vector.quantize_mx(out=v_codes[g, h][:, lo:hi].bitcast(FP8X4), scales=v_scales[g, h][:, lo:hi],
@@ -134,21 +143,16 @@ def tile_attend_spotlight_heads_kernel(tc, query, keys_words, keys_scales, th, r
 
         cast_vals(0, 0, 0, 128, "k_words")
         cast_vals(0, 0, 128, 256, "picked_1")
-        part = sb.tile([P, 1], F32, name="part")
-        minus_one = sb.tile([P, 1], F32, name="minus_one")
-        nc.gpsimd.memset(minus_one[:], -1.0)
-        nc.gpsimd.tensor_tensor(out=part[:], in0=sums[0][:], in1=res_sb[:], op=ALU.add)
-        nc.scalar.activation(out=den[:], in_=sums[1][:], func=ACT.Identity, bias=part[:])
-        nc.gpsimd.tensor_tensor(out=inv[:], in0=den[:], in1=minus_one[:], op=ALU.pow)
         cast_vals(0, 1, 0, 256, "picked_0")
-        cast_vals(1, 0, 0, 256, "v_raw_0_0")
+        cast_vals(1, 0, 0, 256, "sum_1")
 
-        dealt = [sb.tile([P, PACK, P], F32, name="dealt_0"), sb.tile([P, PACK, P], F32, name="dealt_1", tag="v_raw_1_0", align_bytes=64)]
+        dealt = [sb.tile([P, PACK, P], F32, name="dealt_0", tag="dealt_0", align_bytes=64), reuse.tile([P, PACK, P], F32, name="dealt_1", offset=0, align_bytes=64)]
         for g in range(PASSES):
-            dst = dealt[g][:].rearrange("q r (c i) -> q c r i", i=4)
-            src = placed[:, g * K_PASS:(g + 1) * K_PASS].rearrange("q (c i r) -> q c r i", i=4, r=PACK)
+            dst = dealt[g][:].rearrange("q r c -> q c r")
+            src = placed[:, g * K_PASS:(g + 1) * K_PASS].rearrange("q (c r) -> q c r", r=PACK)
             if g == 0:
-                nc.vector.tensor_scalar(out=dst, in0=src, scalar1=inv[:], scalar2=None, op0=ALU.mult)
+                for r in range(0, PACK, 2):
+                    nc.vector.tensor_scalar(out=dst[:, :, r:r + 2], in0=src[:, :, r:r + 2], scalar1=inv[:], scalar2=None, op0=ALU.mult)
             else:
                 nc.scalar.activation(out=dst, in_=src, func=ACT.Copy, scale=inv[:])
             for r in range(PACK):
@@ -160,24 +164,28 @@ def tile_attend_spotlight_heads_kernel(tc, query, keys_words, keys_scales, th, r
         quantize_vals(0, 1, 0, 256)
         quantize_vals(1, 0, 0, 256)
 
-        w_bf = [sb.tile([P, Q, PACK], BF16, name="w_bf_0", tag="picked_0", align_bytes=64), sb.tile([P, Q, PACK], BF16, name="w_bf_1", align_bytes=64)]
-        w_codes = [sb.tile([P, Q], U32, name="w_codes_0", tag="v_raw_1_0", align_bytes=64), sb.tile([P, Q], U32, name="w_codes_1", align_bytes=64)]
+        v_codes[1, 1] = sb.tile([P, E_HALF], U32, name="v_codes_1_1", tag="dealt_0", align_bytes=64)
+        w_bf = [reuse.tile([P, Q, PACK], BF16, name="w_bf_0", offset=2048, align_bytes=64), sb.tile([P, Q, PACK], BF16, name="w_bf_1", align_bytes=64)]
+        w_codes = [sb.tile([P, Q], U32, name="w_codes_0", align_bytes=64), sb.tile([P, Q], U32, name="w_codes_1", align_bytes=64)]
         w_scales = [sb.tile([P, Q], U8, name="w_scales_%d" % g, align_bytes=64) for g in range(PASSES)]
+        out_parts = ((0, 0, 256), (1, 0, 128), (1, 128, 256))
+        out_bank = [ps.tile([P, hi - lo], F32, name="out_bank_%d" % n, tag="score_%d" % n) for n, (h, lo, hi) in enumerate(out_parts)]
         for g in range(PASSES):
             nc.vector.tensor_tensor(out=w_bf[g][:], in0=wt_bank[g][:].rearrange("p r q -> p q r"),
                                     in1=fac_sb[:, g, :].unsqueeze(1).to_broadcast([P, Q, PACK]), op=ALU.mult)
-        out_bank = [ps.tile([P, E_HALF], F32, name="out_bank_%d" % h, tag="score_%d" % h) for h in range(2)]
-        for g in range(PASSES):
-            nc.vector.quantize_mx(out=w_codes[g][:].bitcast(FP8X4), scales=w_scales[g][:], in_=w_bf[g][:].rearrange("p q j -> p (q j)"))
             if g == 0:
                 quantize_vals(1, 1, 0, 256)
-            for h in range(2):
+            nc.vector.quantize_mx(out=w_codes[g][:].bitcast(FP8X4), scales=w_scales[g][:], in_=w_bf[g][:].rearrange("p q j -> p (q j)"))
+            for n, (h, lo, hi) in enumerate(out_parts):
                 nc.tensor.matmul_mx(
-                    out=out_bank[h][:], lhsT=w_codes[g][:].bitcast(FP8X4), lhsT_scale=w_scales[g][:],
-                    rhs=v_codes[g, h][:].bitcast(FP8X4), rhs_scale=v_scales[g, h][:],
+                    out=out_bank[n][:], lhsT=w_codes[g][:].bitcast(FP8X4), lhsT_scale=w_scales[g][:],
+                    rhs=v_codes[g, h][:, lo:hi].bitcast(FP8X4), rhs_scale=v_scales[g, h][:, lo:hi],
                     start=(g == 0), stop=(g == PASSES - 1))
         result = [sb.tile([P, E_HALF], F32, name="result_%d" % h) for h in range(2)]
-        nc.scalar.copy(out=result[0][:], in_=out_bank[0][:])
-        nc.vector.tensor_copy(out=result[1][:], in_=out_bank[1][:])
+        for n, (h, lo, hi) in enumerate(out_parts):
+            if h == 0:
+                nc.scalar.copy(out=result[h][:, lo:hi], in_=out_bank[n][:])
+            else:
+                nc.vector.tensor_copy(out=result[h][:, lo:hi], in_=out_bank[n][:])
         nc.scalar.dma_start(out=out[:, 0:E_HALF], in_=result[0][:])
         nc.sync.dma_start(out=out[:, E_HALF:E], in_=result[1][:])

@@ -21,13 +21,23 @@ P = 128
 PACK = 4
 K_PASS = P * PACK
 PASSES = T // K_PASS
-SCORE_WIDTHS = (256, 256, 256, 128, 128)
+QUADRANTS = 4
+SCALE_ROWS = 4
+ALIGN = 64
+RUN = 4
+LIST_HALF = SLOTS // 2
 E_HALF = E // 2
-HALF = SLOTS // 2
+E_QUARTER = E // 4
+
+Q_ON_VECTOR = 80
+SCORE_WIDTHS = (256, 256, 256, 128, 128)
+SCORE_BANKS_ON_VECTOR = (0, 2)
+V_LOADS = ((0, 0, E), (1, 0, E_HALF), (1, E_HALF, E))
+OUT_PARTS = ((0, 0, E_HALF), (1, 0, E_QUARTER), (1, E_QUARTER, E_HALF))
 
 
 def interleave_views(grouped, raw):
-    return (grouped[:].rearrange("p (c i) t -> p c t i", i=4), raw[:].rearrange("p t (c i) -> p c t i", i=4))
+    return grouped.rearrange("p (c i) r -> p c r i", i=RUN), raw.rearrange("p r (c i) -> p c r i", i=RUN)
 
 
 def tile_attend_spotlight_heads_kernel(tc, query, keys_words, keys_scales, th, reserve, ground, fac, vals, offs, out):
@@ -39,15 +49,14 @@ def tile_attend_spotlight_heads_kernel(tc, query, keys_words, keys_scales, th, r
 
         offsets = sb.tile([P, SLOTS // 16], U16, name="offsets")
         q_raw = sb.tile([P, PACK, Q], F32, name="q_raw")
-        k_words = sb.tile([P, 2 * T], U8, name="k_words", tag="k_words", align_bytes=64)
-        k_scales = sb.tile([P, T], U8, name="k_scales", align_bytes=64)
+        k_words = sb.tile([P, 2 * T], U8, name="k_words", tag="k_words", align_bytes=ALIGN)
+        k_scales = sb.tile([P, T], U8, name="k_scales", align_bytes=ALIGN)
         th_sb = sb.tile([P, 1], F32, name="th_sb")
         res_sb = sb.tile([P, 1], F32, name="res_sb")
         fac_sb = sb.tile([P, PASSES, PACK], F32, name="fac_sb")
         ground_sb = sb.tile([P, T], F32, name="ground_sb")
-        v_parts = ((0, 0, E), (1, 0, E_HALF), (1, E_HALF, E))
         v_raw = [sb.tile([P, PACK, E], F32, name="v_raw_0"),
-                 reuse.tile([P, PACK, E_HALF], F32, name="v_raw_1", offset=0, align_bytes=64),
+                 reuse.tile([P, PACK, E_HALF], F32, name="v_raw_1", offset=0, align_bytes=ALIGN),
                  sb.tile([P, PACK, E_HALF], F32, name="v_raw_2")]
         placed = sb.tile([P, T], F32, name="placed")
         ident = sb.tile([P, P], F32, name="ident")
@@ -56,13 +65,16 @@ def tile_attend_spotlight_heads_kernel(tc, query, keys_words, keys_scales, th, r
         nc.vector.memset(placed[:], 0.0)
 
         def load_vals(n):
-            g, lo, hi = v_parts[n]
-            nc.sync.dma_start(out=v_raw[n][:], in_=vals[g * K_PASS:(g + 1) * K_PASS, lo:hi].rearrange("(p j) e -> p j e", j=PACK))
+            g, lo, hi = V_LOADS[n]
+            rows = vals[g * K_PASS:(g + 1) * K_PASS, lo:hi]
+            nc.sync.dma_start(out=v_raw[n][:], in_=rows.rearrange("(p r) e -> p r e", r=PACK))
 
-        nc.sync.dma_start(out=q_raw[:], in_=query.rearrange("(p j) q -> p j q", j=PACK))
+        nc.sync.dma_start(out=q_raw[:], in_=query.rearrange("(p r) q -> p r q", r=PACK))
         nc.sync.dma_start(out=k_words[:].bitcast(I32), in_=keys_words[0].bitcast(I32))
-        for quad in range(4):
-            nc.sync.dma_start(out=k_scales[32 * quad:32 * quad + 4, :].bitcast(I32), in_=keys_scales[0, 4 * quad:4 * quad + 4, :].bitcast(I32))
+        for quad in range(QUADRANTS):
+            queue = nc.scalar if quad == QUADRANTS - 1 else nc.sync
+            queue.dma_start(out=k_scales[32 * quad:32 * quad + SCALE_ROWS, :].bitcast(I32),
+                            in_=keys_scales[0, SCALE_ROWS * quad:SCALE_ROWS * (quad + 1), :].bitcast(I32))
         nc.sync.dma_start(offsets[:], offs)
         load_vals(0)
         nc.sync.dma_start(out=th_sb[:], in_=th)
@@ -76,46 +88,47 @@ def tile_attend_spotlight_heads_kernel(tc, query, keys_words, keys_scales, th, r
         neg_th = sb.tile([P, 1], F32, name="neg_th")
         nc.gpsimd.tensor_scalar(out=neg_th[:], in0=th_sb[:], scalar1=-1.0, scalar2=0.0, op0=ALU.mult, op1=ALU.add)
 
-        q_bf = sb.tile([P, Q, PACK], BF16, name="q_bf", align_bytes=64)
-        q_codes = sb.tile([P, Q], U32, name="q_codes", align_bytes=64)
-        q_scales = sb.tile([P, Q], U8, name="q_scales", align_bytes=64)
-        dst, src = interleave_views(q_bf, q_raw)
-        nc.vector.tensor_copy(out=dst[:, 0:14], in_=src[:, 0:14])
-        nc.scalar.activation(out=dst[:, 14:32], in_=src[:, 14:32], func=ACT.Copy)
-        nc.vector.quantize_mx(out=q_codes[:].bitcast(FP8X4), scales=q_scales[:], in_=q_bf[:].rearrange("p q j -> p (q j)"))
+        q_bf = sb.tile([P, Q, PACK], BF16, name="q_bf", align_bytes=ALIGN)
+        q_codes = sb.tile([P, Q], U32, name="q_codes", align_bytes=ALIGN)
+        q_scales = sb.tile([P, Q], U8, name="q_scales", align_bytes=ALIGN)
+        q_dst, q_src = interleave_views(q_bf[:], q_raw[:])
+        split, runs = Q_ON_VECTOR // RUN, Q // RUN
+        nc.vector.tensor_copy(out=q_dst[:, 0:split], in_=q_src[:, 0:split])
+        nc.scalar.activation(out=q_dst[:, split:runs], in_=q_src[:, split:runs], func=ACT.Copy)
+        nc.vector.quantize_mx(out=q_codes[:].bitcast(FP8X4), scales=q_scales[:], in_=q_bf[:].rearrange("p q r -> p (q r)"))
 
         a = sb.tile([P, T], F32, name="a")
-        lo = 0
+        first = 0
         for n, width in enumerate(SCORE_WIDTHS):
-            hi = lo + width
+            end = first + width
             bank = ps.tile([P, width], F32, name="score_%d" % n, tag="score_%d" % n)
             nc.tensor.matmul_mx(
                 out=bank[:], lhsT=q_codes[:].bitcast(FP8X4), lhsT_scale=q_scales[:],
-                rhs=k_words[:, 2 * lo:2 * hi].bitcast(FP4X4),
-                rhs_scale=k_scales[:, lo:hi], start=True, stop=True)
-            if n not in (0, 2):
-                nc.scalar.copy(out=a[:, lo:hi], in_=bank[:])
+                rhs=k_words[:, 2 * first:2 * end].bitcast(FP4X4),
+                rhs_scale=k_scales[:, first:end], start=True, stop=True)
+            if n in SCORE_BANKS_ON_VECTOR:
+                nc.vector.tensor_copy(out=a[:, first:end], in_=bank[:])
             else:
-                nc.vector.tensor_copy(out=a[:, lo:hi], in_=bank[:])
-            lo = hi
+                nc.scalar.copy(out=a[:, first:end], in_=bank[:])
+            first = end
 
-        lists = [offsets[:, s * (HALF // 16):(s + 1) * (HALF // 16)] for s in range(2)]
-        picked = [sb.tile([P, HALF], F32, name="picked_%d" % s, tag="picked_%d" % s, align_bytes=64) for s in range(2)]
-        b = [sb.tile([P, HALF], F32, name="b_%d" % s, tag="b_%d" % s, align_bytes=64) for s in range(2)]
-        sums = [sb.tile([P, 1], F32, name="sum_%d" % s, tag="sum_%d" % s, align_bytes=64) for s in range(2)]
+        lists = [offsets[:, s * (LIST_HALF // 16):(s + 1) * (LIST_HALF // 16)] for s in range(2)]
+        picked = [sb.tile([P, LIST_HALF], F32, name="picked_%d" % s, tag="picked_%d" % s, align_bytes=ALIGN) for s in range(2)]
+        b = [sb.tile([P, LIST_HALF], F32, name="b_%d" % s, tag="b_%d" % s, align_bytes=ALIGN) for s in range(2)]
+        sums = [sb.tile([P, 1], F32, name="sum_%d" % s, tag="sum_%d" % s, align_bytes=ALIGN) for s in range(2)]
         for s in range(2):
             nc.vector.tensor_copy(out=picked[s][:], in_=a[:].indirect(lists[s]))
         den = res_sb
         for s in range(2):
             nc.scalar.activation(out=b[s][:], in_=picked[s][:], func=ACT.Relu, bias=neg_th[:], accum_out=sums[s][:])
-            so_far, den = den, sb.tile([P, 1], F32, name="den_%d" % s, tag="den_%d" % s, align_bytes=64)
+            so_far, den = den, sb.tile([P, 1], F32, name="den_%d" % s, tag="den_%d" % s, align_bytes=ALIGN)
             nc.scalar.activation(out=den[:], in_=sums[s][:], func=ACT.Identity, bias=so_far[:])
         minus_one = sb.tile([P, 1], F32, name="minus_one")
         nc.gpsimd.memset(minus_one[:], -1.0)
-        inv = sb.tile([P, 1], F32, name="inv", tag="inv", align_bytes=64)
+        inv = sb.tile([P, 1], F32, name="inv", tag="inv", align_bytes=ALIGN)
         nc.gpsimd.tensor_tensor(out=inv[:], in0=den[:], in1=minus_one[:], op=ALU.pow)
-        nc.vector.tensor_copy(out=placed[:].indirect(lists[0]), in_=b[0][:])
-        nc.vector.tensor_copy(out=placed[:].indirect(lists[1]), in_=b[1][:])
+        for s in range(2):
+            nc.vector.tensor_copy(out=placed[:].indirect(lists[s]), in_=b[s][:])
 
         wt_bank = [ps.tile([P, PACK, Q], F32, name="wt_bank_%d" % g) for g in range(PASSES)]
         for g in range(PASSES):
@@ -126,63 +139,68 @@ def tile_attend_spotlight_heads_kernel(tc, query, keys_words, keys_scales, th, r
         v_codes, v_scales, v_bf = {}, {}, {}
         for g in range(PASSES):
             for h in range(2):
-                v_scales[g, h] = sb.tile([P, E_HALF], U8, name="v_scales_%d_%d" % (g, h), align_bytes=64)
-
-        v_codes[0, 0] = sb.tile([P, E_HALF], U32, name="v_codes_0_0", tag="den_1", align_bytes=64)
-        v_codes[0, 1] = sb.tile([P, E_HALF], U32, name="v_codes_0_1", align_bytes=64)
-        v_codes[1, 0] = sb.tile([P, E_HALF], U32, name="v_codes_1_0", align_bytes=64)
+                v_scales[g, h] = sb.tile([P, E_HALF], U8, name="v_scales_%d_%d" % (g, h), align_bytes=ALIGN)
+        v_codes[0, 0] = sb.tile([P, E_HALF], U32, name="v_codes_0_0", tag="den_1", align_bytes=ALIGN)
+        v_codes[0, 1] = sb.tile([P, E_HALF], U32, name="v_codes_0_1", align_bytes=ALIGN)
+        v_codes[1, 0] = sb.tile([P, E_HALF], U32, name="v_codes_1_0", align_bytes=ALIGN)
 
         def cast_vals(g, h, lo, hi, tag):
-            v_bf[g, h, lo] = sb.tile([P, hi - lo, PACK], BF16, name="v_bf_%d_%d_%d" % (g, h, lo), tag=tag, align_bytes=64)
-            nc.scalar.copy(out=v_bf[g, h, lo][:].rearrange("p (c i) t -> p c t i", i=4),
-                           in_=(v_raw[0][:, :, h * E_HALF + lo:h * E_HALF + hi] if g == 0 else v_raw[1 + h][:]).rearrange("p t (c i) -> p c t i", i=4))
+            v_bf[g, h, lo] = sb.tile([P, hi - lo, PACK], BF16, name="v_bf_%d_%d_%d" % (g, h, lo), tag=tag, align_bytes=ALIGN)
+            raw = v_raw[0][:, :, h * E_HALF + lo:h * E_HALF + hi] if g == 0 else v_raw[1 + h][:]
+            v_dst, v_src = interleave_views(v_bf[g, h, lo][:], raw)
+            nc.scalar.copy(out=v_dst, in_=v_src)
 
         def quantize_vals(g, h, lo, hi):
             nc.vector.quantize_mx(out=v_codes[g, h][:, lo:hi].bitcast(FP8X4), scales=v_scales[g, h][:, lo:hi],
-                                  in_=v_bf[g, h, lo][:].rearrange("p e j -> p (e j)"))
+                                  in_=v_bf[g, h, lo][:].rearrange("p e r -> p (e r)"))
 
-        cast_vals(0, 0, 0, 128, "k_words")
-        cast_vals(0, 0, 128, 256, "picked_1")
-        cast_vals(0, 1, 0, 256, "picked_0")
-        cast_vals(1, 0, 0, 256, "sum_1")
+        cast_vals(0, 0, 0, E_QUARTER, "k_words")
+        cast_vals(0, 0, E_QUARTER, E_HALF, "picked_1")
+        cast_vals(0, 1, 0, E_HALF, "picked_0")
+        cast_vals(1, 0, 0, E_HALF, "sum_1")
 
-        dealt = [sb.tile([P, PACK, P], F32, name="dealt_0", tag="dealt_0", align_bytes=64), reuse.tile([P, PACK, P], F32, name="dealt_1", offset=0, align_bytes=64)]
+        dealt = [sb.tile([P, PACK, P], F32, name="dealt_0", tag="dealt_0", align_bytes=ALIGN),
+                 reuse.tile([P, PACK, P], F32, name="dealt_1", offset=0, align_bytes=ALIGN)]
         for g in range(PASSES):
-            dst = dealt[g][:].rearrange("q r c -> q c r")
-            src = placed[:, g * K_PASS:(g + 1) * K_PASS].rearrange("q (c r) -> q c r", r=PACK)
+            u_dst = dealt[g][:].rearrange("q r p -> q p r")
+            u_src = placed[:, g * K_PASS:(g + 1) * K_PASS].rearrange("q (p r) -> q p r", r=PACK)
             if g == 0:
                 for r in range(0, PACK, 2):
-                    nc.vector.tensor_scalar(out=dst[:, :, r:r + 2], in0=src[:, :, r:r + 2], scalar1=inv[:], scalar2=None, op0=ALU.mult)
+                    nc.vector.tensor_scalar(out=u_dst[:, :, r:r + 2], in0=u_src[:, :, r:r + 2], scalar1=inv[:],
+                                            scalar2=None, op0=ALU.mult)
             else:
-                nc.scalar.activation(out=dst, in_=src, func=ACT.Copy, scale=inv[:])
+                nc.scalar.activation(out=u_dst, in_=u_src, func=ACT.Copy, scale=inv[:])
             for r in range(PACK):
                 nc.tensor.matmul(wt_bank[g][:, r, :], dealt[g][:, r, :], ident[:],
                                  start=False, stop=(r == PACK - 1), is_transpose=True)
-        cast_vals(1, 1, 0, 256, "inv")
-        quantize_vals(0, 0, 0, 128)
-        quantize_vals(0, 0, 128, 256)
-        quantize_vals(0, 1, 0, 256)
-        quantize_vals(1, 0, 0, 256)
+        cast_vals(1, 1, 0, E_HALF, "inv")
+        quantize_vals(0, 0, 0, E_QUARTER)
+        quantize_vals(0, 0, E_QUARTER, E_HALF)
+        quantize_vals(0, 1, 0, E_HALF)
+        quantize_vals(1, 0, 0, E_HALF)
 
-        v_codes[1, 1] = sb.tile([P, E_HALF], U32, name="v_codes_1_1", tag="dealt_0", align_bytes=64)
-        w_bf = [reuse.tile([P, Q, PACK], BF16, name="w_bf_0", offset=2048, align_bytes=64), sb.tile([P, Q, PACK], BF16, name="w_bf_1", align_bytes=64)]
-        w_codes = [sb.tile([P, Q], U32, name="w_codes_0", align_bytes=64), sb.tile([P, Q], U32, name="w_codes_1", align_bytes=64)]
-        w_scales = [sb.tile([P, Q], U8, name="w_scales_%d" % g, align_bytes=64) for g in range(PASSES)]
-        out_parts = ((0, 0, 256), (1, 0, 128), (1, 128, 256))
-        out_bank = [ps.tile([P, hi - lo], F32, name="out_bank_%d" % n, tag="score_%d" % n) for n, (h, lo, hi) in enumerate(out_parts)]
+        v_codes[1, 1] = sb.tile([P, E_HALF], U32, name="v_codes_1_1", tag="dealt_0", align_bytes=ALIGN)
+        w_bf = [reuse.tile([P, Q, PACK], BF16, name="w_bf_0", offset=4 * K_PASS, align_bytes=ALIGN),
+                sb.tile([P, Q, PACK], BF16, name="w_bf_1", align_bytes=ALIGN)]
+        w_codes = [sb.tile([P, Q], U32, name="w_codes_%d" % g, align_bytes=ALIGN) for g in range(PASSES)]
+        w_scales = [sb.tile([P, Q], U8, name="w_scales_%d" % g, align_bytes=ALIGN) for g in range(PASSES)]
+        out_bank = [ps.tile([P, hi - lo], F32, name="out_bank_%d" % n, tag="score_%d" % n)
+                    for n, (h, lo, hi) in enumerate(OUT_PARTS)]
         for g in range(PASSES):
             nc.vector.tensor_tensor(out=w_bf[g][:], in0=wt_bank[g][:].rearrange("p r q -> p q r"),
                                     in1=fac_sb[:, g, :].unsqueeze(1).to_broadcast([P, Q, PACK]), op=ALU.mult)
             if g == 0:
-                quantize_vals(1, 1, 0, 256)
-            nc.vector.quantize_mx(out=w_codes[g][:].bitcast(FP8X4), scales=w_scales[g][:], in_=w_bf[g][:].rearrange("p q j -> p (q j)"))
-            for n, (h, lo, hi) in enumerate(out_parts):
+                quantize_vals(1, 1, 0, E_HALF)
+            nc.vector.quantize_mx(out=w_codes[g][:].bitcast(FP8X4), scales=w_scales[g][:],
+                                  in_=w_bf[g][:].rearrange("p q r -> p (q r)"))
+            for n, (h, lo, hi) in enumerate(OUT_PARTS):
                 nc.tensor.matmul_mx(
                     out=out_bank[n][:], lhsT=w_codes[g][:].bitcast(FP8X4), lhsT_scale=w_scales[g][:],
                     rhs=v_codes[g, h][:, lo:hi].bitcast(FP8X4), rhs_scale=v_scales[g, h][:, lo:hi],
                     start=(g == 0), stop=(g == PASSES - 1))
+
         result = [sb.tile([P, E_HALF], F32, name="result_%d" % h) for h in range(2)]
-        for n, (h, lo, hi) in enumerate(out_parts):
+        for n, (h, lo, hi) in enumerate(OUT_PARTS):
             if h == 0:
                 nc.scalar.copy(out=result[h][:, lo:hi], in_=out_bank[n][:])
             else:

from contextlib import ExitStack

import concourse.mybir as mybir
from concourse.masks import make_identity

D, E, T, Q, SLOTS = 512, 512, 1024, 128, 512
FLOPS = 2 * Q * D * T + 2 * Q * T * E

F32 = mybir.dt.float32
BF16 = mybir.dt.bfloat16
I32 = mybir.dt.int32
U32 = mybir.dt.uint32
U16 = mybir.dt.uint16
U8 = mybir.dt.uint8
FP8X4 = mybir.dt.float8_e4m3fn_x4
FP4X4 = mybir.dt.float4_e2m1fn_x4
ALU = mybir.AluOpType
ACT = mybir.ActivationFunctionType

P = 128
PACK = 4
K_PASS = P * PACK
PASSES = T // K_PASS
QUADRANTS = 4
SCALE_ROWS = 4
ALIGN = 64
RUN = 4
LIST_HALF = SLOTS // 2
E_HALF = E // 2
E_QUARTER = E // 4

Q_ON_VECTOR = 80
SCORE_WIDTHS = (256, 256, 256, 128, 128)
SCORE_BANKS_ON_VECTOR = (0, 2)
V_LOADS = ((0, 0, E), (1, 0, E_HALF), (1, E_HALF, E))
OUT_PARTS = ((0, 0, E_HALF), (1, 0, E_QUARTER), (1, E_QUARTER, E_HALF))


def interleave_views(grouped, raw):
    return grouped.rearrange("p (c i) r -> p c r i", i=RUN), raw.rearrange("p r (c i) -> p c r i", i=RUN)


def tile_attend_spotlight_heads_kernel(tc, query, keys_words, keys_scales, th, reserve, ground, fac, vals, offs, out):
    nc = tc.nc
    with ExitStack() as ctx:
        sb = ctx.enter_context(tc.tile_pool(name="sb", bufs=1))
        reuse = ctx.enter_context(tc.tile_pool(name="reuse", bufs=1))
        ps = ctx.enter_context(tc.psum_pool(name="ps", bufs=1))

        offsets = sb.tile([P, SLOTS // 16], U16, name="offsets")
        q_raw = sb.tile([P, PACK, Q], F32, name="q_raw")
        k_words = sb.tile([P, 2 * T], U8, name="k_words", tag="k_words", align_bytes=ALIGN)
        k_scales = sb.tile([P, T], U8, name="k_scales", align_bytes=ALIGN)
        th_sb = sb.tile([P, 1], F32, name="th_sb")
        res_sb = sb.tile([P, 1], F32, name="res_sb")
        fac_sb = sb.tile([P, PASSES, PACK], F32, name="fac_sb")
        ground_sb = sb.tile([P, T], F32, name="ground_sb")
        v_raw = [sb.tile([P, PACK, E], F32, name="v_raw_0"),
                 reuse.tile([P, PACK, E_HALF], F32, name="v_raw_1", offset=0, align_bytes=ALIGN),
                 sb.tile([P, PACK, E_HALF], F32, name="v_raw_2")]
        placed = sb.tile([P, T], F32, name="placed")
        ident = sb.tile([P, P], F32, name="ident")

        nc.gpsimd.memset(k_scales[:].bitcast(I32), 0)
        nc.vector.memset(placed[:], 0.0)

        def load_vals(n):
            g, lo, hi = V_LOADS[n]
            rows = vals[g * K_PASS:(g + 1) * K_PASS, lo:hi]
            nc.sync.dma_start(out=v_raw[n][:], in_=rows.rearrange("(p r) e -> p r e", r=PACK))

        nc.sync.dma_start(out=q_raw[:], in_=query.rearrange("(p r) q -> p r q", r=PACK))
        nc.sync.dma_start(out=k_words[:].bitcast(I32), in_=keys_words[0].bitcast(I32))
        for quad in range(QUADRANTS):
            queue = nc.scalar if quad == QUADRANTS - 1 else nc.sync
            queue.dma_start(out=k_scales[32 * quad:32 * quad + SCALE_ROWS, :].bitcast(I32),
                            in_=keys_scales[0, SCALE_ROWS * quad:SCALE_ROWS * (quad + 1), :].bitcast(I32))
        nc.sync.dma_start(offsets[:], offs)
        load_vals(0)
        nc.sync.dma_start(out=th_sb[:], in_=th)
        nc.sync.dma_start(out=res_sb[:], in_=reserve)
        nc.sync.dma_start(out=ground_sb[:], in_=ground)
        load_vals(1)
        load_vals(2)
        nc.sync.dma_start(out=fac_sb[:], in_=fac.rearrange("o (g p r) -> p (o g) r", p=P, r=PACK))
        make_identity(nc, ident[:])

        neg_th = sb.tile([P, 1], F32, name="neg_th")
        nc.gpsimd.tensor_scalar(out=neg_th[:], in0=th_sb[:], scalar1=-1.0, scalar2=0.0, op0=ALU.mult, op1=ALU.add)

        q_bf = sb.tile([P, Q, PACK], BF16, name="q_bf", align_bytes=ALIGN)
        q_codes = sb.tile([P, Q], U32, name="q_codes", align_bytes=ALIGN)
        q_scales = sb.tile([P, Q], U8, name="q_scales", align_bytes=ALIGN)
        q_dst, q_src = interleave_views(q_bf[:], q_raw[:])
        split, runs = Q_ON_VECTOR // RUN, Q // RUN
        nc.vector.tensor_copy(out=q_dst[:, 0:split], in_=q_src[:, 0:split])
        nc.scalar.activation(out=q_dst[:, split:runs], in_=q_src[:, split:runs], func=ACT.Copy)
        nc.vector.quantize_mx(out=q_codes[:].bitcast(FP8X4), scales=q_scales[:], in_=q_bf[:].rearrange("p q r -> p (q r)"))

        a = sb.tile([P, T], F32, name="a")
        first = 0
        for n, width in enumerate(SCORE_WIDTHS):
            end = first + width
            bank = ps.tile([P, width], F32, name="score_%d" % n, tag="score_%d" % n)
            nc.tensor.matmul_mx(
                out=bank[:], lhsT=q_codes[:].bitcast(FP8X4), lhsT_scale=q_scales[:],
                rhs=k_words[:, 2 * first:2 * end].bitcast(FP4X4),
                rhs_scale=k_scales[:, first:end], start=True, stop=True)
            if n in SCORE_BANKS_ON_VECTOR:
                nc.vector.tensor_copy(out=a[:, first:end], in_=bank[:])
            else:
                nc.scalar.copy(out=a[:, first:end], in_=bank[:])
            first = end

        lists = [offsets[:, s * (LIST_HALF // 16):(s + 1) * (LIST_HALF // 16)] for s in range(2)]
        picked = [sb.tile([P, LIST_HALF], F32, name="picked_%d" % s, tag="picked_%d" % s, align_bytes=ALIGN) for s in range(2)]
        b = [sb.tile([P, LIST_HALF], F32, name="b_%d" % s, tag="b_%d" % s, align_bytes=ALIGN) for s in range(2)]
        sums = [sb.tile([P, 1], F32, name="sum_%d" % s, tag="sum_%d" % s, align_bytes=ALIGN) for s in range(2)]
        for s in range(2):
            nc.vector.tensor_copy(out=picked[s][:], in_=a[:].indirect(lists[s]))
        den = res_sb
        for s in range(2):
            nc.scalar.activation(out=b[s][:], in_=picked[s][:], func=ACT.Relu, bias=neg_th[:], accum_out=sums[s][:])
            so_far, den = den, sb.tile([P, 1], F32, name="den_%d" % s, tag="den_%d" % s, align_bytes=ALIGN)
            nc.scalar.activation(out=den[:], in_=sums[s][:], func=ACT.Identity, bias=so_far[:])
        minus_one = sb.tile([P, 1], F32, name="minus_one")
        nc.gpsimd.memset(minus_one[:], -1.0)
        inv = sb.tile([P, 1], F32, name="inv", tag="inv", align_bytes=ALIGN)
        nc.gpsimd.tensor_tensor(out=inv[:], in0=den[:], in1=minus_one[:], op=ALU.pow)
        for s in range(2):
            nc.vector.tensor_copy(out=placed[:].indirect(lists[s]), in_=b[s][:])

        wt_bank = [ps.tile([P, PACK, Q], F32, name="wt_bank_%d" % g) for g in range(PASSES)]
        for g in range(PASSES):
            for r in range(PACK):
                nc.tensor.matmul(wt_bank[g][:, r, :], ground_sb[:, g * K_PASS + r:(g + 1) * K_PASS:PACK], ident[:],
                                 start=(r == 0), stop=False, is_transpose=True)

        v_codes, v_scales, v_bf = {}, {}, {}
        for g in range(PASSES):
            for h in range(2):
                v_scales[g, h] = sb.tile([P, E_HALF], U8, name="v_scales_%d_%d" % (g, h), align_bytes=ALIGN)
        v_codes[0, 0] = sb.tile([P, E_HALF], U32, name="v_codes_0_0", tag="den_1", align_bytes=ALIGN)
        v_codes[0, 1] = sb.tile([P, E_HALF], U32, name="v_codes_0_1", align_bytes=ALIGN)
        v_codes[1, 0] = sb.tile([P, E_HALF], U32, name="v_codes_1_0", align_bytes=ALIGN)

        def cast_vals(g, h, lo, hi, tag):
            v_bf[g, h, lo] = sb.tile([P, hi - lo, PACK], BF16, name="v_bf_%d_%d_%d" % (g, h, lo), tag=tag, align_bytes=ALIGN)
            raw = v_raw[0][:, :, h * E_HALF + lo:h * E_HALF + hi] if g == 0 else v_raw[1 + h][:]
            v_dst, v_src = interleave_views(v_bf[g, h, lo][:], raw)
            nc.scalar.copy(out=v_dst, in_=v_src)

        def quantize_vals(g, h, lo, hi):
            nc.vector.quantize_mx(out=v_codes[g, h][:, lo:hi].bitcast(FP8X4), scales=v_scales[g, h][:, lo:hi],
                                  in_=v_bf[g, h, lo][:].rearrange("p e r -> p (e r)"))

        cast_vals(0, 0, 0, E_QUARTER, "k_words")
        cast_vals(0, 0, E_QUARTER, E_HALF, "picked_1")
        cast_vals(0, 1, 0, E_HALF, "picked_0")
        cast_vals(1, 0, 0, E_HALF, "sum_1")

        dealt = [sb.tile([P, PACK, P], F32, name="dealt_0", tag="dealt_0", align_bytes=ALIGN),
                 reuse.tile([P, PACK, P], F32, name="dealt_1", offset=0, align_bytes=ALIGN)]
        for g in range(PASSES):
            u_dst = dealt[g][:].rearrange("q r p -> q p r")
            u_src = placed[:, g * K_PASS:(g + 1) * K_PASS].rearrange("q (p r) -> q p r", r=PACK)
            if g == 0:
                for r in range(0, PACK, 2):
                    nc.vector.tensor_scalar(out=u_dst[:, :, r:r + 2], in0=u_src[:, :, r:r + 2], scalar1=inv[:],
                                            scalar2=None, op0=ALU.mult)
            else:
                nc.scalar.activation(out=u_dst, in_=u_src, func=ACT.Copy, scale=inv[:])
            for r in range(PACK):
                nc.tensor.matmul(wt_bank[g][:, r, :], dealt[g][:, r, :], ident[:],
                                 start=False, stop=(r == PACK - 1), is_transpose=True)
        cast_vals(1, 1, 0, E_HALF, "inv")
        quantize_vals(0, 0, 0, E_QUARTER)
        quantize_vals(0, 0, E_QUARTER, E_HALF)
        quantize_vals(0, 1, 0, E_HALF)
        quantize_vals(1, 0, 0, E_HALF)

        v_codes[1, 1] = sb.tile([P, E_HALF], U32, name="v_codes_1_1", tag="dealt_0", align_bytes=ALIGN)
        w_bf = [reuse.tile([P, Q, PACK], BF16, name="w_bf_0", offset=4 * K_PASS, align_bytes=ALIGN),
                sb.tile([P, Q, PACK], BF16, name="w_bf_1", align_bytes=ALIGN)]
        w_codes = [sb.tile([P, Q], U32, name="w_codes_%d" % g, align_bytes=ALIGN) for g in range(PASSES)]
        w_scales = [sb.tile([P, Q], U8, name="w_scales_%d" % g, align_bytes=ALIGN) for g in range(PASSES)]
        out_bank = [ps.tile([P, hi - lo], F32, name="out_bank_%d" % n, tag="score_%d" % n)
                    for n, (h, lo, hi) in enumerate(OUT_PARTS)]
        for g in range(PASSES):
            nc.vector.tensor_tensor(out=w_bf[g][:], in0=wt_bank[g][:].rearrange("p r q -> p q r"),
                                    in1=fac_sb[:, g, :].unsqueeze(1).to_broadcast([P, Q, PACK]), op=ALU.mult)
            if g == 0:
                quantize_vals(1, 1, 0, E_HALF)
            nc.vector.quantize_mx(out=w_codes[g][:].bitcast(FP8X4), scales=w_scales[g][:],
                                  in_=w_bf[g][:].rearrange("p q r -> p (q r)"))
            for n, (h, lo, hi) in enumerate(OUT_PARTS):
                nc.tensor.matmul_mx(
                    out=out_bank[n][:], lhsT=w_codes[g][:].bitcast(FP8X4), lhsT_scale=w_scales[g][:],
                    rhs=v_codes[g, h][:, lo:hi].bitcast(FP8X4), rhs_scale=v_scales[g, h][:, lo:hi],
                    start=(g == 0), stop=(g == PASSES - 1))

        result = [sb.tile([P, E_HALF], F32, name="result_%d" % h) for h in range(2)]
        for n, (h, lo, hi) in enumerate(OUT_PARTS):
            if h == 0:
                nc.scalar.copy(out=result[h][:, lo:hi], in_=out_bank[n][:])
            else:
                nc.vector.tensor_copy(out=result[h][:, lo:hi], in_=out_bank[n][:])
        nc.scalar.dma_start(out=out[:, 0:E_HALF], in_=result[0][:])
        nc.sync.dma_start(out=out[:, E_HALF:E], in_=result[1][:])
